import numpy as np
import ml_dtypes


def mxq(x, axis, fmt="e4m3"):
    dtype, down = {"e4m3": (ml_dtypes.float8_e4m3fn, 7), "e5m2": (ml_dtypes.float8_e5m2, 14)}[fmt]
    v = np.moveaxis(np.asarray(x, np.float32).astype(ml_dtypes.bfloat16).astype(np.float64), axis, -1)
    blocks = v.reshape(v.shape[:-1] + (-1, 32))
    amax = np.abs(blocks).max(-1, keepdims=True)
    byte = np.maximum(np.where(amax > 0, np.frexp(amax)[1] - 1 + 127, 0) - down, 1)
    scale = np.exp2(byte - 127.0)
    codes = (blocks / scale).astype(np.float32).astype(dtype).astype(np.float64)
    return np.moveaxis((codes * scale).reshape(v.shape), -1, axis)


WIDE = False


def mx_kscale(k):
    if not WIDE:
        return np.ones(k)
    levels = np.array([10, -10, 5, -5, 0])
    if k % 512:
        return np.exp2(np.random.permutation(np.resize(levels, k // 32))).repeat(32)
    a = np.empty((k // 512, 16))
    for p in range(k // 512):
        a[p, :8] = np.random.permutation(np.resize(levels, 8))
        for g in range(8):
            far = levels[np.abs(levels - a[p, g]) >= 10]
            a[p, g + 8] = far[np.random.randint(len(far))]
    return np.exp2(a.ravel()).repeat(32)


def f64(x):
    return np.asarray(x).astype(np.float64)


def striped(idx):
    return np.tile(idx.reshape(-1, 16).T, (8, 1)).astype(np.uint16)


def unstriped(offs):
    return offs[:16].T.reshape(-1).astype(np.int64)


def striped8(idx):
    return np.concatenate([x.reshape(-1, 16).T for x in idx]).astype(np.uint16)


def runs(offs, k):
    lists = np.stack([offs[16 * r : 16 * r + 16].T.reshape(-1) for r in range(8)]).astype(np.int64)
    return lists[np.arange(k) % 512 // 64]


def pack_weight(w):
    k, n = w.shape
    w = f64(np.asarray(w, np.float32).astype(ml_dtypes.bfloat16)).reshape(k // 32, 32, n)
    amax = np.abs(w).max(1)
    byte = np.clip(np.where(amax > 0, np.frexp(amax)[1] - 1 + 127 - 7, 1), 1, 254)
    scaled = (w * np.exp2(127.0 - byte)[:, None, :]).reshape(k, n).astype(np.float32)
    words = np.ascontiguousarray(scaled.reshape(k // 512, 128, 4, n).transpose(0, 1, 3, 2)).astype(ml_dtypes.float8_e4m3fn).view(np.uint8)
    return words, np.ascontiguousarray(byte.astype(np.uint8).reshape(k // 512, 16, n))


def unpack_weight(words, scales):
    g, p, n, _ = words.shape
    vals = np.ascontiguousarray(words).view(ml_dtypes.float8_e4m3fn).astype(np.float64) * np.repeat(np.exp2(scales.astype(np.float64) - 127.0), 8, axis=1)[..., None]
    return vals.transpose(0, 1, 3, 2).reshape(g * 512, n)


K, T, S, V, N = 512, 2048, 512, 512, 512
P = 2 ** 7


def setup_inputs():
    n = np.random.standard_normal
    s = mx_kscale(K)[:, None]
    packed_xT = pack_weight(n((K, T)) * s)
    return {
        "x_words": packed_xT[0],
        "x_scales": packed_xT[1],
        "w1": (n((K, N)) / np.sqrt(K) / s).astype(np.float32),
        "w2": (n((K, N)) / np.sqrt(K) / s).astype(np.float32),
        "pi1": np.tile(np.random.uniform(0.2, 0.8, S), (P, 1)).astype(np.float32),
        "pi2": np.tile(np.random.uniform(0.2, 0.8, S), (P, 1)).astype(np.float32),
        "offs": striped(np.random.permutation(T)[:S]),
        "cen": striped(np.random.permutation(T)[:V]),
        "k1": striped8(np.random.randint(0, V, (8, S))),
        "k2": striped8(np.random.randint(0, V, (8, S))),
    }


def reference(x_words, x_scales, w1, w2, pi1, pi2, offs, cen, k1, k2):
    xq = unpack_weight(x_words, x_scales)[:, unstriped(offs)]
    y = mxq(f64(w1), 0, "e4m3").T @ xq
    x_cen = unpack_weight(x_words, x_scales)[:, unstriped(cen)]
    c = mxq(f64(w2), 0, "e4m3").T @ x_cen
    return np.log(f64(pi1)[:1] * (np.exp(-0.125 * ((y - (c[np.arange(N)[:, None], runs(k1, N)])) ** 2))) + f64(pi2)[:1] * (np.exp(-0.125 * ((y - (c[np.arange(N)[:, None], runs(k2, N)])) ** 2))))

@@ -1,0 +1,213 @@
+import math
+from contextlib import ExitStack
+
+import concourse.mybir as mybir
+from concourse.masks import make_identity
+
+K, T, S, V, N = 512, 2048, 512, 512, 512
+FLOPS = 2 * K * N * (S + V)
+
+F32 = mybir.dt.float32
+BF16 = mybir.dt.bfloat16
+I32 = mybir.dt.int32
+U32 = mybir.dt.uint32
+U16 = mybir.dt.uint16
+U8 = mybir.dt.uint8
+FP8X4 = mybir.dt.float8_e4m3fn_x4
+ACT = mybir.ActivationFunctionType
+ALU = mybir.AluOpType
+
+P = 128
+PACK = 4
+TILES = N // P
+BLOCKS = S // P
+HALF = N // 2
+CLAMP = 24.0
+
+
+def tile_picked_gmm8_none_p_kernel(tc, x_words, x_scales, w1, w2, pi1, pi2, offs, cen, k1, k2, out):
+    nc = tc.nc
+    with ExitStack() as ctx:
+        lists = ctx.enter_context(tc.tile_pool(name="lists", bufs=1))
+        keep = ctx.enter_context(tc.tile_pool(name="keep", bufs=1))
+        psum = ctx.enter_context(tc.psum_pool(name="psum", bufs=1))
+
+        def load_list(name, src):
+            tile = lists.tile([P, S // 16], U16, name=name)
+            nc.sync.dma_start(tile[:], src)
+            return tile
+
+        def load_weight(name, w, c0, c1):
+            raw = keep.tile([P, PACK, c1 - c0], F32, name=name)
+            nc.sync.dma_start(raw[:], w.rearrange("(p j) c -> p j c", j=PACK)[:, :, c0:c1])
+            return raw
+
+        table_scales = keep.tile([P, T], U8, name="table_scales")
+        nc.vector.memset(table_scales[:].bitcast(I32), 0)
+        cen_list = load_list("cen_list", cen)
+        offs_list = load_list("offs_list", offs)
+        k1_list = load_list("k1_list", k1)
+        k2_list = load_list("k2_list", k2)
+        table_words = keep.tile([P, T], I32, name="table_words")
+        nc.sync.dma_start(table_words[:], x_words[0].rearrange("p n t -> p (n t)").bitcast(I32))
+        w2_raw = load_weight("w2_raw", w2, 0, N)
+        w1_raw = [load_weight("w1_raw%d" % h, w1, h * HALF, (h + 1) * HALF) for h in range(2)]
+        for q in range(4):
+            nc.scalar.dma_start(table_scales[32 * q : 32 * q + 4, :].bitcast(I32), x_scales[0, 4 * q : 4 * q + 4, :].bitcast(I32))
+
+        ident = keep.tile([P, P], F32, name="ident")
+        make_identity(nc, ident[:])
+        windows = [keep.tile([P, 2 * V if t < TILES - 1 else V], F32, name="window%d" % t) for t in range(TILES)]
+        for t in range(TILES - 1):
+            nc.gpsimd.memset(windows[t][:, V:], 0.0)
+        pi_rows = keep.tile([P, P], F32, name="pi_rows")
+        nc.gpsimd.memset(pi_rows[:], 0.0)
+        nc.gpsimd.dma_start(pi_rows[0:BLOCKS, :], pi1[0].rearrange("(b q) -> b q", q=P))
+        nc.gpsimd.dma_start(pi_rows[BLOCKS : 2 * BLOCKS, :], pi2[0].rearrange("(b q) -> b q", q=P))
+
+        def gather_words(name, offsets):
+            words = keep.tile([P, S], U32, name=name, align_bytes=64)
+            nc.vector.tensor_copy(words[:], table_words[:].bitcast(U32).indirect(offsets[:]))
+            return words
+
+        def gather_scales(name, offsets):
+            scales = keep.tile([P, S], U8, name=name, align_bytes=64)
+            nc.vector.tensor_copy(scales[:], table_scales[:].indirect(offsets[:]))
+            return scales
+
+        def cast(copy, grouped, raw, m0, m1):
+            dst = grouped[:].rearrange("p (t m j) -> p m j t", t=TILES, j=PACK)[:, m0:m1]
+            copy(dst, raw[:].rearrange("p j (m t) -> p m j t", t=TILES))
+
+        def quantize(grouped, words, scales, t0, t1):
+            nc.vector.quantize_mx(
+                out=words[:, t0 * P : t1 * P].bitcast(FP8X4),
+                scales=scales[:, t0 * P : t1 * P],
+                in_=grouped[:, t0 * P * PACK : t1 * P * PACK],
+            )
+
+        def product(bank, w_words, w_scales, t, words, scales):
+            nc.tensor.matmul_mx(
+                out=bank[:],
+                lhsT=w_words[:, t * P : (t + 1) * P].bitcast(FP8X4),
+                lhsT_scale=w_scales[:, t * P : (t + 1) * P],
+                rhs=words[:].bitcast(FP8X4),
+                rhs_scale=scales[:],
+                start=True,
+                stop=True,
+            )
+
+        cen_words = gather_words("cen_words", cen_list)
+        x_w = gather_words("x_w", offs_list)
+        cen_scales = gather_scales("cen_scales", cen_list)
+        x_s = gather_scales("x_s", offs_list)
+        w2_grouped = keep.tile([P, N * PACK], BF16, name="w2_grouped", align_bytes=64)
+        w2_words = keep.tile([P, N], U32, name="w2_words", align_bytes=64)
+        w2_scales = keep.tile([P, N], U8, name="w2_scales", align_bytes=64)
+        w1_grouped = keep.tile([P, N * PACK], BF16, name="w1_grouped", align_bytes=64)
+        w1_words = keep.tile([P, N], U32, name="w1_words", align_bytes=64)
+        w1_scales = keep.tile([P, N], U8, name="w1_scales", align_bytes=64)
+        cast(nc.scalar.copy, w2_grouped, w2_raw, 0, P)
+        quantize(w2_grouped, w2_words, w2_scales, 0, 2)
+        cast(nc.scalar.copy, w1_grouped, w1_raw[0], 0, P // 2)
+        cast(nc.vector.tensor_copy, w1_grouped, w1_raw[1], P // 2, P)
+        quantize(w1_grouped, w1_words, w1_scales, 0, 1)
+        quantize(w1_grouped, w1_words, w1_scales, 1, 2)
+        quantize(w2_grouped, w2_words, w2_scales, 2, 4)
+        quantize(w1_grouped, w1_words, w1_scales, 2, 4)
+        c_tags = ("a0", "a1", "a2", "a3")
+        y_tags = ("a1", "a2", "a3", "b0")
+        ys = [keep.tile([P, S], F32, name="y%d" % t) for t in range(TILES)]
+
+        def project_c(t):
+            c_bank = psum.tile([P, V], F32, name="c_bank%d" % t, tag=c_tags[t])
+            product(c_bank, w2_words, w2_scales, t, cen_words, cen_scales)
+            nc.scalar.copy(windows[t][:, :V], c_bank[:])
+
+        def project_y(t):
+            y_bank = psum.tile([P, S], F32, name="y_bank%d" % t, tag=y_tags[t])
+            product(y_bank, w1_words, w1_scales, t, x_w, x_s)
+            nc.scalar.copy(ys[t][:], y_bank[:])
+
+        project_c(0)
+        project_y(0)
+        for t in range(1, TILES):
+            project_y(t)
+            project_c(t)
+
+        pi_bank = psum.tile([P, P], F32, name="pi_bank", tag="b0")
+        nc.tensor.transpose(pi_bank[:], pi_rows[:], ident[:])
+        pi_columns = keep.tile([P, 2 * BLOCKS], F32, name="pi_columns")
+        nc.scalar.copy(pi_columns[:], pi_bank[:, : 2 * BLOCKS])
+
+        units = ((0, 0, 4), (1, 0, 4), (2, 0, 2), (2, 2, 4), (3, 0, 2), (3, 2, 3), (3, 3, 4))
+        s2 = keep.tile([P, TILES, S], F32, name="s2")
+        neg_s1 = keep.tile([P, TILES, S], F32, name="neg_s1")
+        d1 = keep.tile([P, TILES, S], F32, name="d1")
+        d2 = keep.tile([P, TILES, S], F32, name="d2")
+        rests = keep.tile([P, TILES, S], F32, name="rests")
+        expo = keep.tile([P, BLOCKS, TILES, P], F32, name="expo")
+        exp_clamp = keep.tile([P, 1], F32, name="exp_clamp", tag="after_exp")
+        last_clamp = keep.tile([P, 1], F32, name="last_clamp")
+        relu_clamps = [s2[:, t, b0 * P : b0 * P + 1] for t, b0, b1 in units[2:]] + [last_clamp[:]] * 2
+        for column in relu_clamps[:-1] + [exp_clamp[:]]:
+            nc.gpsimd.memset(column, CLAMP)
+        sums = [psum.tile([P, TILES, P], F32, name="sum_bank%d" % b, tag="a%d" % b) for b in range(BLOCKS)]
+
+        def difference(d, offsets, u):
+            t, b0, b1 = units[u]
+            cols = slice(b0 * P, b1 * P)
+            nc.vector.tensor_tensor(d[:, t, cols], windows[t][:].indirect(offsets[:, b0 * P // 16 : b1 * P // 16]), ys[t][:, cols], ALU.subtract)
+
+        def exponential(u):
+            t, b0, b1 = units[u]
+            rest = rests[:, t, b0 * P : b1 * P].rearrange("p (b m) -> p b m", m=P)
+            nc.scalar.activation(expo[:, b0:b1, t, :], rest, ACT.Exp, bias=exp_clamp[:], scale=-1.0)
+
+        def squares(u):
+            t, b0, b1 = units[u]
+            cols = slice(b0 * P, b1 * P)
+            if u + 1 < len(units):
+                difference(d1, k1_list, u + 1)
+            nc.vector.scalar_tensor_tensor(neg_s1[:, t, cols], d1[:, t, cols], -0.125, d1[:, t, cols], ALU.mult, ALU.mult)
+            difference(d2, k2_list, u)
+            nc.scalar.activation(s2[:, t, cols], d2[:, t, cols], ACT.Square, scale=math.sqrt(0.125))
+            gap = psum.tile([P, (b1 - b0) * P], F32, name="gap_bank%d" % u, tag="gap%d" % (u % 2))
+            for source, first in ((s2, True), (neg_s1, False)):
+                for b in range(b0, b1):
+                    nc.tensor.matmul(
+                        gap[:, (b - b0) * P : (b - b0 + 1) * P], source[:, t, b * P : (b + 1) * P], ident[:],
+                        start=(first and b == b0), stop=(not first and b == b1 - 1), is_transpose=True)
+            return gap
+
+        def clamped(u, gap):
+            t, b0, b1 = units[u]
+            nc.scalar.activation(rests[:, t, b0 * P : b1 * P], gap[:], ACT.Relu, bias=relu_clamps[u])
+            exponential(u)
+            for b in range(b0, b1):
+                nc.tensor.matmul(sums[b][:, t, :], rests[:, t, b * P : (b + 1) * P], ident[:], start=(t == 0), stop=False, is_transpose=True)
+
+        difference(d1, k1_list, 0)
+        gaps = [squares(0)]
+        for u in range(len(units)):
+            if u + 1 < len(units):
+                gaps.append(squares(u + 1))
+            clamped(u, gaps[u])
+
+        out_rows = out.rearrange("(p t) j -> p t j", t=TILES)
+        logs = keep.tile([P, BLOCKS, TILES, P], F32, name="logs", tag="after_exp")
+
+        def finish(b, t0, t1):
+            result = keep.tile([P, t1 - t0, P], F32, name="result%d_%d" % (b, t0))
+            nc.vector.scalar_tensor_tensor(result[:], sums[b][:, t0:t1, :], -CLAMP, s2[:, t0:t1, b * P : (b + 1) * P], ALU.add, ALU.subtract)
+            nc.sync.dma_start(out_rows[:, t0:t1, b * P : (b + 1) * P], result[:])
+
+        for b in range(BLOCKS):
+            nc.scalar.activation(logs[:, b], expo[:, b], ACT.Ln, bias=pi_columns[:, b : b + 1], scale=pi_columns[:, BLOCKS + b : BLOCKS + b + 1])
+            for t in range(TILES):
+                nc.tensor.matmul(sums[b][:, t, :], logs[:, b, t, :], ident[:], start=False, stop=(t == TILES - 1), is_transpose=True)
+            if b < BLOCKS - 1:
+                finish(b, 0, 4)
+            else:
+                finish(b, 0, 2)
+                finish(b, 2, 4)

@@ -38,32 +38,47 @@ def tile_picked_gmm8_none_p_kernel(tc, x_words, x_scales, w1, w2, pi1, pi2, offs
             return tile
 
         def load_weight(name, w, c0, c1):
-            raw = keep.tile([P, PACK, c1 - c0], F32, name=name)
+            raw = keep.tile([P, PACK, c1 - c0], F32, name=name, tag=name, align_bytes=64)
             nc.sync.dma_start(raw[:], w.rearrange("(p j) c -> p j c", j=PACK)[:, :, c0:c1])
             return raw
 
+        pi_rows = keep.tile([P, P], F32, name="pi_rows")
+        nc.gpsimd.memset(pi_rows[:], 0.0)
+        nc.gpsimd.dma_start(pi_rows[0:BLOCKS, :], pi1[0].rearrange("(b q) -> b q", q=P))
+        nc.scalar.dma_start(pi_rows[BLOCKS : 2 * BLOCKS, :], pi2[0].rearrange("(b q) -> b q", q=P))
         table_scales = keep.tile([P, T], U8, name="table_scales")
         nc.vector.memset(table_scales[:].bitcast(I32), 0)
         cen_list = load_list("cen_list", cen)
         offs_list = load_list("offs_list", offs)
         k1_list = load_list("k1_list", k1)
-        k2_list = load_list("k2_list", k2)
         table_words = keep.tile([P, T], I32, name="table_words")
         nc.sync.dma_start(table_words[:], x_words[0].rearrange("p n t -> p (n t)").bitcast(I32))
         w2_raw = load_weight("w2_raw", w2, 0, N)
-        w1_raw = [load_weight("w1_raw%d" % h, w1, h * HALF, (h + 1) * HALF) for h in range(2)]
+        w1_raw = load_weight("w1_raw", w1, 0, N)
+        k2_list = load_list("k2_list", k2)
         for q in range(4):
             nc.scalar.dma_start(table_scales[32 * q : 32 * q + 4, :].bitcast(I32), x_scales[0, 4 * q : 4 * q + 4, :].bitcast(I32))
 
         ident = keep.tile([P, P], F32, name="ident")
         make_identity(nc, ident[:])
-        windows = [keep.tile([P, 2 * V if t < TILES - 1 else V], F32, name="window%d" % t) for t in range(TILES)]
+        windows = [keep.tile([P, 2 * V if t < TILES - 1 else V], F32, name="window%d" % t, tag="window%d" % t) for t in range(TILES)]
         for t in range(TILES - 1):
-            nc.gpsimd.memset(windows[t][:, V:], 0.0)
-        pi_rows = keep.tile([P, P], F32, name="pi_rows")
-        nc.gpsimd.memset(pi_rows[:], 0.0)
-        nc.gpsimd.dma_start(pi_rows[0:BLOCKS, :], pi1[0].rearrange("(b q) -> b q", q=P))
-        nc.gpsimd.dma_start(pi_rows[BLOCKS : 2 * BLOCKS, :], pi2[0].rearrange("(b q) -> b q", q=P))
+            nc.vector.memset(windows[t][:, V:], 0.0)
+
+        pi_bank = psum.tile([P, P], F32, name="pi_bank", tag="x")
+        nc.tensor.transpose(pi_bank[:], pi_rows[:], ident[:])
+        exp_bias = keep.tile([P, BLOCKS], F32, name="exp_bias", tag="after_exp")
+        nc.scalar.activation(exp_bias[:], pi_bank[:, BLOCKS : 2 * BLOCKS], ACT.Ln, scale=math.exp(CLAMP))
+        p1_columns = keep.tile([P, BLOCKS], F32, name="p1_columns")
+        nc.scalar.copy(p1_columns[:], pi_bank[:, :BLOCKS])
+        grouped = keep.tile([P, 2 * N * PACK - 256], BF16, name="grouped", align_bytes=64)
+        w1_grouped = grouped[:, : N * PACK]
+        w2_grouped = grouped[:, N * PACK - 256 :]
+        nc.scalar.activation(grouped[:, 0 : 2 * N * PACK - 256 : 2 * N * PACK - 257], p1_columns[:, 0:2], ACT.Exp, bias=exp_bias[:, 0:1], scale=-1.0)
+        sums = [psum.tile([P, BLOCKS, P], F32, name="sum_bank%d" % t, tag="a%d" % t) for t in range(TILES)]
+        for t in range(TILES):
+            for b in range(BLOCKS):
+                nc.tensor.matmul(sums[t][:, b, :], p1_columns[:, b : b + 1].to_broadcast([P, P]), ident[:], start=(b == 0), stop=False, is_transpose=True)
 
         def gather_words(name, offsets):
             words = keep.tile([P, S], U32, name=name, align_bytes=64)
@@ -76,23 +91,21 @@ def tile_picked_gmm8_none_p_kernel(tc, x_words, x_scales, w1, w2, pi1, pi2, offs
             return scales
 
         def cast(copy, grouped, raw, m0, m1):
-            dst = grouped[:].rearrange("p (t m j) -> p m j t", t=TILES, j=PACK)[:, m0:m1]
-            copy(dst, raw[:].rearrange("p j (m t) -> p m j t", t=TILES))
+            dst = grouped.rearrange("p (t m j) -> p m j t", t=TILES, j=PACK)[:, m0:m1]
+            copy(dst, raw[:].rearrange("p j (m t) -> p m j t", t=TILES)[:, m0:m1])
 
-        def quantize(grouped, words, scales, t0, t1):
-            nc.vector.quantize_mx(
-                out=words[:, t0 * P : t1 * P].bitcast(FP8X4),
-                scales=scales[:, t0 * P : t1 * P],
-                in_=grouped[:, t0 * P * PACK : t1 * P * PACK],
-            )
+        def quantize(words, scales, grouped, t0, t1):
+            n = (t1 - t0) * P
+            nc.vector.quantize_mx(out=words[:, :n].bitcast(FP8X4), scales=scales[:, :n], in_=grouped[:, t0 * P * PACK : t1 * P * PACK])
+            return [(words[:, i * P : (i + 1) * P], scales[:, i * P : (i + 1) * P]) for i in range(t1 - t0)]
 
-        def product(bank, w_words, w_scales, t, words, scales):
+        def product(bank, weights, words, scales, j0, j1):
             nc.tensor.matmul_mx(
-                out=bank[:],
-                lhsT=w_words[:, t * P : (t + 1) * P].bitcast(FP8X4),
-                lhsT_scale=w_scales[:, t * P : (t + 1) * P],
-                rhs=words[:].bitcast(FP8X4),
-                rhs_scale=scales[:],
+                out=bank[:, j0:j1],
+                lhsT=weights[0].bitcast(FP8X4),
+                lhsT_scale=weights[1],
+                rhs=words[:, j0:j1].bitcast(FP8X4),
+                rhs_scale=scales[:, j0:j1],
                 start=True,
                 stop=True,
             )
@@ -101,68 +114,56 @@ def tile_picked_gmm8_none_p_kernel(tc, x_words, x_scales, w1, w2, pi1, pi2, offs
         x_w = gather_words("x_w", offs_list)
         cen_scales = gather_scales("cen_scales", cen_list)
         x_s = gather_scales("x_s", offs_list)
-        w2_grouped = keep.tile([P, N * PACK], BF16, name="w2_grouped", align_bytes=64)
-        w2_words = keep.tile([P, N], U32, name="w2_words", align_bytes=64)
+        cast(nc.scalar.copy, w2_grouped, w2_raw, 0, P)
+        w2_first = keep.tile([P, P], U32, name="w2_first", align_bytes=64)
         w2_scales = keep.tile([P, N], U8, name="w2_scales", align_bytes=64)
-        w1_grouped = keep.tile([P, N * PACK], BF16, name="w1_grouped", align_bytes=64)
+        w2_tiles = quantize(w2_first[:], w2_scales[:], w2_grouped, 0, 1)
+        cast(nc.scalar.copy, w1_grouped, w1_raw, 0, 48)
+        cast(nc.vector.tensor_copy, w1_grouped, w1_raw, 48, P)
         w1_words = keep.tile([P, N], U32, name="w1_words", align_bytes=64)
         w1_scales = keep.tile([P, N], U8, name="w1_scales", align_bytes=64)
-        cast(nc.scalar.copy, w2_grouped, w2_raw, 0, P)
-        quantize(w2_grouped, w2_words, w2_scales, 0, 2)
-        cast(nc.scalar.copy, w1_grouped, w1_raw[0], 0, P // 2)
-        cast(nc.vector.tensor_copy, w1_grouped, w1_raw[1], P // 2, P)
-        quantize(w1_grouped, w1_words, w1_scales, 0, 1)
-        quantize(w1_grouped, w1_words, w1_scales, 1, 2)
-        quantize(w2_grouped, w2_words, w2_scales, 2, 4)
-        quantize(w1_grouped, w1_words, w1_scales, 2, 4)
-        c_tags = ("a0", "a1", "a2", "a3")
-        y_tags = ("a1", "a2", "a3", "b0")
+        w2_rest = keep.tile([P, N - P], U32, name="w2_rest", tag="w1_raw", align_bytes=64)
+        w1_tiles = quantize(w1_words[:], w1_scales[:], w1_grouped, 0, 1)
+        w1_tiles = w1_tiles + quantize(w1_words[:, P:], w1_scales[:, P:], w1_grouped, 1, 2)
+        w2_tiles = w2_tiles + quantize(w2_rest[:], w2_scales[:, P:], w2_grouped, 1, 2)
+        w1_tiles = w1_tiles + quantize(w1_words[:, 2 * P :], w1_scales[:, 2 * P :], w1_grouped, 2, 4)
+        w2_tiles = w2_tiles + quantize(w2_rest[:, P:], w2_scales[:, 2 * P :], w2_grouped, 2, 4)
         ys = [keep.tile([P, S], F32, name="y%d" % t) for t in range(TILES)]
 
         def project_c(t):
-            c_bank = psum.tile([P, V], F32, name="c_bank%d" % t, tag=c_tags[t])
-            product(c_bank, w2_words, w2_scales, t, cen_words, cen_scales)
+            c_bank = psum.tile([P, V], F32, name="c_bank%d" % t, tag="x")
+            product(c_bank, w2_tiles[t], cen_words, cen_scales, 0, V)
             nc.scalar.copy(windows[t][:, :V], c_bank[:])
 
-        def project_y(t):
-            y_bank = psum.tile([P, S], F32, name="y_bank%d" % t, tag=y_tags[t])
-            product(y_bank, w1_words, w1_scales, t, x_w, x_s)
-            nc.scalar.copy(ys[t][:], y_bank[:])
+        def project_y(t, j0, j1, tag):
+            y_bank = psum.tile([P, S], F32, name="y_bank%d_%d" % (t, j0), tag=tag)
+            product(y_bank, w1_tiles[t], x_w, x_s, j0, j1)
+            nc.scalar.copy(ys[t][:, j0:j1], y_bank[:, j0:j1])
 
         project_c(0)
-        project_y(0)
+        project_y(0, 0, S // 2, "gap0")
+        project_y(0, S // 2, S, "gap1")
         for t in range(1, TILES):
-            project_y(t)
+            project_y(t, 0, S, "y")
             project_c(t)
 
-        pi_bank = psum.tile([P, P], F32, name="pi_bank", tag="b0")
-        nc.tensor.transpose(pi_bank[:], pi_rows[:], ident[:])
-        pi_columns = keep.tile([P, 2 * BLOCKS], F32, name="pi_columns")
-        nc.scalar.copy(pi_columns[:], pi_bank[:, : 2 * BLOCKS])
 
-        units = ((0, 0, 4), (1, 0, 4), (2, 0, 2), (2, 2, 4), (3, 0, 2), (3, 2, 3), (3, 3, 4))
+        units = ((0, 0, 2), (0, 2, 4), (1, 0, 4), (2, 0, 2), (2, 2, 4), (3, 0, 2), (3, 2, 3), (3, 3, 4))
         s2 = keep.tile([P, TILES, S], F32, name="s2")
         neg_s1 = keep.tile([P, TILES, S], F32, name="neg_s1")
         d1 = keep.tile([P, TILES, S], F32, name="d1")
         d2 = keep.tile([P, TILES, S], F32, name="d2")
         rests = keep.tile([P, TILES, S], F32, name="rests")
-        expo = keep.tile([P, BLOCKS, TILES, P], F32, name="expo")
-        exp_clamp = keep.tile([P, 1], F32, name="exp_clamp", tag="after_exp")
+        expo = keep.tile([P, TILES, S], F32, name="expo")
         last_clamp = keep.tile([P, 1], F32, name="last_clamp")
         relu_clamps = [s2[:, t, b0 * P : b0 * P + 1] for t, b0, b1 in units[2:]] + [last_clamp[:]] * 2
-        for column in relu_clamps[:-1] + [exp_clamp[:]]:
-            nc.gpsimd.memset(column, CLAMP)
-        sums = [psum.tile([P, TILES, P], F32, name="sum_bank%d" % b, tag="a%d" % b) for b in range(BLOCKS)]
+        for column in relu_clamps[:-1]:
+            nc.vector.memset(column, CLAMP)
 
         def difference(d, offsets, u):
             t, b0, b1 = units[u]
             cols = slice(b0 * P, b1 * P)
             nc.vector.tensor_tensor(d[:, t, cols], windows[t][:].indirect(offsets[:, b0 * P // 16 : b1 * P // 16]), ys[t][:, cols], ALU.subtract)
-
-        def exponential(u):
-            t, b0, b1 = units[u]
-            rest = rests[:, t, b0 * P : b1 * P].rearrange("p (b m) -> p b m", m=P)
-            nc.scalar.activation(expo[:, b0:b1, t, :], rest, ACT.Exp, bias=exp_clamp[:], scale=-1.0)
 
         def squares(u):
             t, b0, b1 = units[u]
@@ -183,9 +184,10 @@ def tile_picked_gmm8_none_p_kernel(tc, x_words, x_scales, w1, w2, pi1, pi2, offs
         def clamped(u, gap):
             t, b0, b1 = units[u]
             nc.scalar.activation(rests[:, t, b0 * P : b1 * P], gap[:], ACT.Relu, bias=relu_clamps[u])
-            exponential(u)
             for b in range(b0, b1):
-                nc.tensor.matmul(sums[b][:, t, :], rests[:, t, b * P : (b + 1) * P], ident[:], start=(t == 0), stop=False, is_transpose=True)
+                block = slice(b * P, (b + 1) * P)
+                nc.scalar.activation(expo[:, t, block], rests[:, t, block], ACT.Exp, bias=exp_bias[:, b : b + 1], scale=-1.0)
+                nc.tensor.matmul(sums[t][:, b, :], expo[:, t, block], ident[:], start=False, stop=(b == BLOCKS - 1), is_transpose=True)
 
         difference(d1, k1_list, 0)
         gaps = [squares(0)]
@@ -195,19 +197,14 @@ def tile_picked_gmm8_none_p_kernel(tc, x_words, x_scales, w1, w2, pi1, pi2, offs
             clamped(u, gaps[u])
 
         out_rows = out.rearrange("(p t) j -> p t j", t=TILES)
-        logs = keep.tile([P, BLOCKS, TILES, P], F32, name="logs", tag="after_exp")
-
-        def finish(b, t0, t1):
-            result = keep.tile([P, t1 - t0, P], F32, name="result%d_%d" % (b, t0))
-            nc.vector.scalar_tensor_tensor(result[:], sums[b][:, t0:t1, :], -CLAMP, s2[:, t0:t1, b * P : (b + 1) * P], ALU.add, ALU.subtract)
-            nc.sync.dma_start(out_rows[:, t0:t1, b * P : (b + 1) * P], result[:])
-
-        for b in range(BLOCKS):
-            nc.scalar.activation(logs[:, b], expo[:, b], ACT.Ln, bias=pi_columns[:, b : b + 1], scale=pi_columns[:, BLOCKS + b : BLOCKS + b + 1])
-            for t in range(TILES):
-                nc.tensor.matmul(sums[b][:, t, :], logs[:, b, t, :], ident[:], start=False, stop=(t == TILES - 1), is_transpose=True)
-            if b < BLOCKS - 1:
-                finish(b, 0, 4)
-            else:
-                finish(b, 0, 2)
-                finish(b, 2, 4)
+        shifted = keep.tile([P, TILES, S], F32, name="shifted", tag="window3")
+        base = keep.tile([P, TILES, S], F32, name="base")
+        for t0, t1 in ((0, TILES - 1), (TILES - 1, TILES)):
+            nc.vector.tensor_scalar(shifted[:, t0:t1, :], s2[:, t0:t1, :], -1.0, -CLAMP, ALU.mult, ALU.add)
+            nc.vector.tensor_tensor(base[:, t0:t1, :], neg_s1[:, t0:t1, :], shifted[:, t0:t1, :], ALU.max)
+        logs = keep.tile([P, TILES, S], F32, name="logs", tag="after_exp")
+        result = keep.tile([P, TILES, S], F32, name="result")
+        for t, j0, j1 in ((0, 0, S), (1, 0, S), (2, 0, S), (3, 0, 3 * P), (3, 3 * P, S)):
+            nc.scalar.activation(logs[:, t, j0:j1], sums[t][:].rearrange("p b m -> p (b m)")[:, j0:j1], ACT.Ln)
+            nc.vector.tensor_tensor(result[:, t, j0:j1], logs[:, t, j0:j1], base[:, t, j0:j1], ALU.add)
+            nc.sync.dma_start(out_rows[:, t, j0:j1], result[:, t, j0:j1])

import math
from contextlib import ExitStack

import concourse.mybir as mybir
from concourse.masks import make_identity

K, T, S, V, N = 512, 2048, 512, 512, 512
FLOPS = 2 * K * N * (S + V)

F32 = mybir.dt.float32
BF16 = mybir.dt.bfloat16
I32 = mybir.dt.int32
U32 = mybir.dt.uint32
U16 = mybir.dt.uint16
U8 = mybir.dt.uint8
FP8X4 = mybir.dt.float8_e4m3fn_x4
ACT = mybir.ActivationFunctionType
ALU = mybir.AluOpType

P = 128
PACK = 4
TILES = N // P
BLOCKS = S // P
HALF = N // 2
CLAMP = 24.0


def tile_picked_gmm8_none_p_kernel(tc, x_words, x_scales, w1, w2, pi1, pi2, offs, cen, k1, k2, out):
    nc = tc.nc
    with ExitStack() as ctx:
        lists = ctx.enter_context(tc.tile_pool(name="lists", bufs=1))
        keep = ctx.enter_context(tc.tile_pool(name="keep", bufs=1))
        psum = ctx.enter_context(tc.psum_pool(name="psum", bufs=1))

        def load_list(name, src):
            tile = lists.tile([P, S // 16], U16, name=name)
            nc.sync.dma_start(tile[:], src)
            return tile

        def load_weight(name, w, c0, c1):
            raw = keep.tile([P, PACK, c1 - c0], F32, name=name, tag=name, align_bytes=64)
            nc.sync.dma_start(raw[:], w.rearrange("(p j) c -> p j c", j=PACK)[:, :, c0:c1])
            return raw

        pi_rows = keep.tile([P, P], F32, name="pi_rows")
        nc.gpsimd.memset(pi_rows[:], 0.0)
        nc.gpsimd.dma_start(pi_rows[0:BLOCKS, :], pi1[0].rearrange("(b q) -> b q", q=P))
        nc.scalar.dma_start(pi_rows[BLOCKS : 2 * BLOCKS, :], pi2[0].rearrange("(b q) -> b q", q=P))
        table_scales = keep.tile([P, T], U8, name="table_scales")
        nc.vector.memset(table_scales[:].bitcast(I32), 0)
        cen_list = load_list("cen_list", cen)
        offs_list = load_list("offs_list", offs)
        k1_list = load_list("k1_list", k1)
        table_words = keep.tile([P, T], I32, name="table_words")
        nc.sync.dma_start(table_words[:], x_words[0].rearrange("p n t -> p (n t)").bitcast(I32))
        w2_raw = load_weight("w2_raw", w2, 0, N)
        w1_raw = load_weight("w1_raw", w1, 0, N)
        k2_list = load_list("k2_list", k2)
        for q in range(4):
            nc.scalar.dma_start(table_scales[32 * q : 32 * q + 4, :].bitcast(I32), x_scales[0, 4 * q : 4 * q + 4, :].bitcast(I32))

        ident = keep.tile([P, P], F32, name="ident")
        make_identity(nc, ident[:])
        windows = [keep.tile([P, 2 * V if t < TILES - 1 else V], F32, name="window%d" % t, tag="window%d" % t) for t in range(TILES)]
        for t in range(TILES - 1):
            nc.vector.memset(windows[t][:, V:], 0.0)

        pi_bank = psum.tile([P, P], F32, name="pi_bank", tag="x")
        nc.tensor.transpose(pi_bank[:], pi_rows[:], ident[:])
        exp_bias = keep.tile([P, BLOCKS], F32, name="exp_bias", tag="after_exp")
        nc.scalar.activation(exp_bias[:], pi_bank[:, BLOCKS : 2 * BLOCKS], ACT.Ln, scale=math.exp(CLAMP))
        p1_columns = keep.tile([P, BLOCKS], F32, name="p1_columns")
        nc.scalar.copy(p1_columns[:], pi_bank[:, :BLOCKS])
        grouped = keep.tile([P, 2 * N * PACK - 256], BF16, name="grouped", align_bytes=64)
        w1_grouped = grouped[:, : N * PACK]
        w2_grouped = grouped[:, N * PACK - 256 :]
        nc.scalar.activation(grouped[:, 0 : 2 * N * PACK - 256 : 2 * N * PACK - 257], p1_columns[:, 0:2], ACT.Exp, bias=exp_bias[:, 0:1], scale=-1.0)
        sums = [psum.tile([P, BLOCKS, P], F32, name="sum_bank%d" % t, tag="a%d" % t) for t in range(TILES)]
        for t in range(TILES):
            for b in range(BLOCKS):
                nc.tensor.matmul(sums[t][:, b, :], p1_columns[:, b : b + 1].to_broadcast([P, P]), ident[:], start=(b == 0), stop=False, is_transpose=True)

        def gather_words(name, offsets):
            words = keep.tile([P, S], U32, name=name, align_bytes=64)
            nc.vector.tensor_copy(words[:], table_words[:].bitcast(U32).indirect(offsets[:]))
            return words

        def gather_scales(name, offsets):
            scales = keep.tile([P, S], U8, name=name, align_bytes=64)
            nc.vector.tensor_copy(scales[:], table_scales[:].indirect(offsets[:]))
            return scales

        def cast(copy, grouped, raw, m0, m1):
            dst = grouped.rearrange("p (t m j) -> p m j t", t=TILES, j=PACK)[:, m0:m1]
            copy(dst, raw[:].rearrange("p j (m t) -> p m j t", t=TILES)[:, m0:m1])

        def quantize(words, scales, grouped, t0, t1):
            n = (t1 - t0) * P
            nc.vector.quantize_mx(out=words[:, :n].bitcast(FP8X4), scales=scales[:, :n], in_=grouped[:, t0 * P * PACK : t1 * P * PACK])
            return [(words[:, i * P : (i + 1) * P], scales[:, i * P : (i + 1) * P]) for i in range(t1 - t0)]

        def product(bank, weights, words, scales, j0, j1):
            nc.tensor.matmul_mx(
                out=bank[:, j0:j1],
                lhsT=weights[0].bitcast(FP8X4),
                lhsT_scale=weights[1],
                rhs=words[:, j0:j1].bitcast(FP8X4),
                rhs_scale=scales[:, j0:j1],
                start=True,
                stop=True,
            )

        cen_words = gather_words("cen_words", cen_list)
        x_w = gather_words("x_w", offs_list)
        cen_scales = gather_scales("cen_scales", cen_list)
        x_s = gather_scales("x_s", offs_list)
        cast(nc.scalar.copy, w2_grouped, w2_raw, 0, P)
        w2_first = keep.tile([P, P], U32, name="w2_first", align_bytes=64)
        w2_scales = keep.tile([P, N], U8, name="w2_scales", align_bytes=64)
        w2_tiles = quantize(w2_first[:], w2_scales[:], w2_grouped, 0, 1)
        cast(nc.scalar.copy, w1_grouped, w1_raw, 0, 48)
        cast(nc.vector.tensor_copy, w1_grouped, w1_raw, 48, P)
        w1_words = keep.tile([P, N], U32, name="w1_words", align_bytes=64)
        w1_scales = keep.tile([P, N], U8, name="w1_scales", align_bytes=64)
        w2_rest = keep.tile([P, N - P], U32, name="w2_rest", tag="w1_raw", align_bytes=64)
        w1_tiles = quantize(w1_words[:], w1_scales[:], w1_grouped, 0, 1)
        w1_tiles = w1_tiles + quantize(w1_words[:, P:], w1_scales[:, P:], w1_grouped, 1, 2)
        w2_tiles = w2_tiles + quantize(w2_rest[:], w2_scales[:, P:], w2_grouped, 1, 2)
        w1_tiles = w1_tiles + quantize(w1_words[:, 2 * P :], w1_scales[:, 2 * P :], w1_grouped, 2, 4)
        w2_tiles = w2_tiles + quantize(w2_rest[:, P:], w2_scales[:, 2 * P :], w2_grouped, 2, 4)
        ys = [keep.tile([P, S], F32, name="y%d" % t) for t in range(TILES)]

        def project_c(t):
            c_bank = psum.tile([P, V], F32, name="c_bank%d" % t, tag="x")
            product(c_bank, w2_tiles[t], cen_words, cen_scales, 0, V)
            nc.scalar.copy(windows[t][:, :V], c_bank[:])

        def project_y(t, j0, j1, tag):
            y_bank = psum.tile([P, S], F32, name="y_bank%d_%d" % (t, j0), tag=tag)
            product(y_bank, w1_tiles[t], x_w, x_s, j0, j1)
            nc.scalar.copy(ys[t][:, j0:j1], y_bank[:, j0:j1])

        project_c(0)
        project_y(0, 0, S // 2, "gap0")
        project_y(0, S // 2, S, "gap1")
        for t in range(1, TILES):
            project_y(t, 0, S, "y")
            project_c(t)


        units = ((0, 0, 2), (0, 2, 4), (1, 0, 4), (2, 0, 2), (2, 2, 4), (3, 0, 2), (3, 2, 3), (3, 3, 4))
        s2 = keep.tile([P, TILES, S], F32, name="s2")
        neg_s1 = keep.tile([P, TILES, S], F32, name="neg_s1")
        d1 = keep.tile([P, TILES, S], F32, name="d1")
        d2 = keep.tile([P, TILES, S], F32, name="d2")
        rests = keep.tile([P, TILES, S], F32, name="rests")
        expo = keep.tile([P, TILES, S], F32, name="expo")
        last_clamp = keep.tile([P, 1], F32, name="last_clamp")
        relu_clamps = [s2[:, t, b0 * P : b0 * P + 1] for t, b0, b1 in units[2:]] + [last_clamp[:]] * 2
        for column in relu_clamps[:-1]:
            nc.vector.memset(column, CLAMP)

        def difference(d, offsets, u):
            t, b0, b1 = units[u]
            cols = slice(b0 * P, b1 * P)
            nc.vector.tensor_tensor(d[:, t, cols], windows[t][:].indirect(offsets[:, b0 * P // 16 : b1 * P // 16]), ys[t][:, cols], ALU.subtract)

        def squares(u):
            t, b0, b1 = units[u]
            cols = slice(b0 * P, b1 * P)
            if u + 1 < len(units):
                difference(d1, k1_list, u + 1)
            nc.vector.scalar_tensor_tensor(neg_s1[:, t, cols], d1[:, t, cols], -0.125, d1[:, t, cols], ALU.mult, ALU.mult)
            difference(d2, k2_list, u)
            nc.scalar.activation(s2[:, t, cols], d2[:, t, cols], ACT.Square, scale=math.sqrt(0.125))
            gap = psum.tile([P, (b1 - b0) * P], F32, name="gap_bank%d" % u, tag="gap%d" % (u % 2))
            for source, first in ((s2, True), (neg_s1, False)):
                for b in range(b0, b1):
                    nc.tensor.matmul(
                        gap[:, (b - b0) * P : (b - b0 + 1) * P], source[:, t, b * P : (b + 1) * P], ident[:],
                        start=(first and b == b0), stop=(not first and b == b1 - 1), is_transpose=True)
            return gap

        def clamped(u, gap):
            t, b0, b1 = units[u]
            nc.scalar.activation(rests[:, t, b0 * P : b1 * P], gap[:], ACT.Relu, bias=relu_clamps[u])
            for b in range(b0, b1):
                block = slice(b * P, (b + 1) * P)
                nc.scalar.activation(expo[:, t, block], rests[:, t, block], ACT.Exp, bias=exp_bias[:, b : b + 1], scale=-1.0)
                nc.tensor.matmul(sums[t][:, b, :], expo[:, t, block], ident[:], start=False, stop=(b == BLOCKS - 1), is_transpose=True)

        difference(d1, k1_list, 0)
        gaps = [squares(0)]
        for u in range(len(units)):
            if u + 1 < len(units):
                gaps.append(squares(u + 1))
            clamped(u, gaps[u])

        out_rows = out.rearrange("(p t) j -> p t j", t=TILES)
        shifted = keep.tile([P, TILES, S], F32, name="shifted", tag="window3")
        base = keep.tile([P, TILES, S], F32, name="base")
        for t0, t1 in ((0, TILES - 1), (TILES - 1, TILES)):
            nc.vector.tensor_scalar(shifted[:, t0:t1, :], s2[:, t0:t1, :], -1.0, -CLAMP, ALU.mult, ALU.add)
            nc.vector.tensor_tensor(base[:, t0:t1, :], neg_s1[:, t0:t1, :], shifted[:, t0:t1, :], ALU.max)
        logs = keep.tile([P, TILES, S], F32, name="logs", tag="after_exp")
        result = keep.tile([P, TILES, S], F32, name="result")
        for t, j0, j1 in ((0, 0, S), (1, 0, S), (2, 0, S), (3, 0, 3 * P), (3, 3 * P, S)):
            nc.scalar.activation(logs[:, t, j0:j1], sums[t][:].rearrange("p b m -> p (b m)")[:, j0:j1], ACT.Ln)
            nc.vector.tensor_tensor(result[:, t, j0:j1], logs[:, t, j0:j1], base[:, t, j0:j1], ALU.add)
            nc.sync.dma_start(out_rows[:, t, j0:j1], result[:, t, j0:j1])
